import numpy as np
import ml_dtypes


def mxq(x, axis, fmt="e4m3"):
    dtype, down = {"e4m3": (ml_dtypes.float8_e4m3fn, 7), "e5m2": (ml_dtypes.float8_e5m2, 14)}[fmt]
    v = np.moveaxis(np.asarray(x, np.float32).astype(ml_dtypes.bfloat16).astype(np.float64), axis, -1)
    blocks = v.reshape(v.shape[:-1] + (-1, 32))
    amax = np.abs(blocks).max(-1, keepdims=True)
    byte = np.maximum(np.where(amax > 0, np.frexp(amax)[1] - 1 + 127, 0) - down, 1)
    scale = np.exp2(byte - 127.0)
    codes = (blocks / scale).astype(np.float32).astype(dtype).astype(np.float64)
    return np.moveaxis((codes * scale).reshape(v.shape), -1, axis)


WIDE = False


def mx_kscale(k):
    if not WIDE:
        return np.ones(k)
    levels = np.array([10, -10, 5, -5, 0])
    if k % 512:
        return np.exp2(np.random.permutation(np.resize(levels, k // 32))).repeat(32)
    a = np.empty((k // 512, 16))
    for p in range(k // 512):
        a[p, :8] = np.random.permutation(np.resize(levels, 8))
        for g in range(8):
            far = levels[np.abs(levels - a[p, g]) >= 10]
            a[p, g + 8] = far[np.random.randint(len(far))]
    return np.exp2(a.ravel()).repeat(32)


def f64(x):
    return np.asarray(x).astype(np.float64)


def striped(idx):
    return np.tile(idx.reshape(-1, 16).T, (8, 1)).astype(np.uint16)


def unstriped(offs):
    return offs[:16].T.reshape(-1).astype(np.int64)


def striped8(idx):
    return np.concatenate([x.reshape(-1, 16).T for x in idx]).astype(np.uint16)


def runs(offs, k):
    lists = np.stack([offs[16 * r : 16 * r + 16].T.reshape(-1) for r in range(8)]).astype(np.int64)
    return lists[np.arange(k) % 512 // 64]


def pack_weight(w):
    k, n = w.shape
    w = f64(np.asarray(w, np.float32).astype(ml_dtypes.bfloat16)).reshape(k // 32, 32, n)
    amax = np.abs(w).max(1)
    byte = np.clip(np.where(amax > 0, np.frexp(amax)[1] - 1 + 127 - 7, 1), 1, 254)
    scaled = (w * np.exp2(127.0 - byte)[:, None, :]).reshape(k, n).astype(np.float32)
    words = np.ascontiguousarray(scaled.reshape(k // 512, 128, 4, n).transpose(0, 1, 3, 2)).astype(ml_dtypes.float8_e4m3fn).view(np.uint8)
    return words, np.ascontiguousarray(byte.astype(np.uint8).reshape(k // 512, 16, n))


def unpack_weight(words, scales):
    g, p, n, _ = words.shape
    vals = np.ascontiguousarray(words).view(ml_dtypes.float8_e4m3fn).astype(np.float64) * np.repeat(np.exp2(scales.astype(np.float64) - 127.0), 8, axis=1)[..., None]
    return vals.transpose(0, 1, 3, 2).reshape(g * 512, n)


K, T, S, N, G, H, W = 512, 1024, 256, 512, 2048, 512, 128


def setup_inputs():
    n = np.random.standard_normal
    s = mx_kscale(K)[:, None]
    u = mx_kscale(K)
    packed_xT = pack_weight(n((K, T)) * s)
    packed_dT = pack_weight(n((K, G)) / s)
    packed_w1 = pack_weight(n((H, N)) / np.sqrt(2 * H) / u[:, None])
    packed_w2 = pack_weight(n((K, N)) / np.sqrt(2 * K) / s)
    perm = np.random.permutation(S)
    perm2 = np.random.permutation(S)
    return {
        "x_words": packed_xT[0],
        "x_scales": packed_xT[1],
        "d_words": packed_dT[0],
        "d_scales": packed_dT[1],
        "gn": (np.random.uniform(0.5, 1.5, (H, 1)) * u[:, None]).astype(np.float32),
        "w1_words": packed_w1[0],
        "w1_scales": packed_w1[1],
        "w2_words": packed_w2[0],
        "w2_scales": packed_w2[1],
        "offs": striped(np.random.permutation(T)[:S]),
        "k1": striped8(np.random.randint(0, G, (8, H))),
        "n1": striped(perm[:W]),
        "n2": striped(perm[W:]),
        "n3": striped(np.random.permutation(S)),
        "hz": striped8(np.random.randint(0, T, (8, S))),
        "n4": striped(perm2[:W]),
        "n5": striped(perm2[W:]),
    }


def reference(x_words, x_scales, d_words, d_scales, gn, w1_words, w1_scales, w2_words, w2_scales, offs, k1, n1, n2, n3, hz, n4, n5):
    d_k1 = unpack_weight(d_words, d_scales)[np.arange(K)[:, None], runs(k1, K)]
    xq = unpack_weight(x_words, x_scales)[:, unstriped(offs)]
    h = 0.0625 * (d_k1.T @ xq)
    pa = h[:, unstriped(n1)]
    pb = h[:, unstriped(n2)]
    ra = np.maximum(pa, pb)
    ds = h.copy()
    ds[:, unstriped(n1)] = ra
    z = f64(gn) * (ds - ds[:, unstriped(n3)])
    x_hz = unpack_weight(x_words, x_scales)[np.arange(K)[:, None], runs(hz, K)]
    h2 = unpack_weight(w1_words, w1_scales).T @ mxq(z, 0, "e4m3") + unpack_weight(w2_words, w2_scales).T @ x_hz
    pa2 = h2[:, unstriped(n4)]
    pb2 = h2[:, unstriped(n5)]
    rb = np.maximum(pa2, pb2)
    ra2 = pa2 / (np.abs(pb2) + 0.5)
    ds2 = np.zeros((N, S))
    ds2[:, unstriped(n4)] = ra2
    out = ds2.copy()
    out[:, unstriped(n5)] = rb
    return out

@@ -1,0 +1,238 @@
+from contextlib import ExitStack
+
+import concourse.mybir as mybir
+
+K, T, S, N, G, H, W = 512, 1024, 256, 512, 2048, 512, 128
+FLOPS = 2 * S * (K * H + H * N + K * N)
+
+F32 = mybir.dt.float32
+BF16 = mybir.dt.bfloat16
+I32 = mybir.dt.int32
+U32 = mybir.dt.uint32
+U16 = mybir.dt.uint16
+U8 = mybir.dt.uint8
+FP8X4 = mybir.dt.float8_e4m3fn_x4
+ALU = mybir.AluOpType
+COPY = mybir.ActivationFunctionType.Copy
+
+P = 128
+PACK = 4
+TILES = 4
+HALF = S // 2
+
+
+def tile_picked_pqmhfillmratio_none_p_kernel(
+    tc, x_words, x_scales, d_words, d_scales, gn, w1_words, w1_scales, w2_words, w2_scales,
+    offs, k1, n1, n2, n3, hz, n4, n5, out,
+):
+    nc = tc.nc
+    with ExitStack() as ctx:
+        sb = ctx.enter_context(tc.tile_pool(name="sb", bufs=1))
+        psum = ctx.enter_context(tc.psum_pool(name="psum", bufs=1))
+
+        def tile(name, shape, dtype, tag=""):
+            return sb.tile(shape, dtype, name=name, align_bytes=64, tag=tag or name)
+
+        def load_list(name, src):
+            dst = tile(name, list(src.shape), U16)
+            nc.sync.dma_start(dst[:], src)
+            return dst
+
+        def load_words(name, src):
+            dst = tile(name, [P, src.shape[2]], U32)
+            nc.sync.dma_start(dst[:].bitcast(I32), src[0].rearrange("p n t -> p (n t)").bitcast(I32))
+            return dst
+
+        def gather_codes(name, table, offsets, count, dtype):
+            dst = tile(name, [P, count], dtype)
+            nc.vector.tensor_copy(dst[:], table[:].indirect(offsets[:]))
+            return dst
+
+        def place_odd_runs(plane):
+            for e in range(2):
+                nc.scalar.dma_start(plane[2 + e : P : 32, :].bitcast(I32), plane[16 + e : P : 32, :].bitcast(I32))
+
+        def deal(name, src, dtype):
+            dst = tile(name, [P, H], dtype)
+            nc.vector.tensor_copy(
+                dst[:].rearrange("p (t c i) -> p c t i", t=PACK, i=4),
+                src[:].rearrange("p (c i t) -> p c t i", t=PACK, i=4),
+            )
+            return dst
+
+        d_table_s = tile("d_table_s", [P, G], U8)
+        x_table_s = tile("x_table_s", [P, T], U8)
+        for table in (d_table_s, x_table_s):
+            half = table.shape[1] // 2
+            nc.vector.memset(table[:, :half].bitcast(I32), 0)
+            nc.gpsimd.memset(table[:, half:].bitcast(I32), 0)
+
+        k1_t = load_list("k1_t", k1)
+        offs_t = load_list("offs_t", offs)
+        n1_t = load_list("n1_t", n1)
+        for e in range(2):
+            nc.sync.dma_start(d_table_s[e:P:16, :].bitcast(I32), d_scales[0].bitcast(I32)[e:16:2, :])
+        d_table_w = load_words("d_table_w", d_words)
+        for e in range(2):
+            nc.sync.dma_start(x_table_s[e:P:16, :].bitcast(I32), x_scales[0].bitcast(I32)[e:16:2, :])
+        for e in range(2):
+            nc.sync.dma_start(x_table_s[2 + e : P : 32, :].bitcast(I32), x_scales[0].bitcast(I32)[2 + e : 16 : 4, :])
+        x_table_w = load_words("x_table_w", x_words)
+
+        d_picked_s = gather_codes("d_picked_s", d_table_s, k1_t, H, U8)
+        d_s = deal("d_s", d_picked_s, U8)
+        place_odd_runs(d_s)
+        d_picked_w = gather_codes("d_picked_w", d_table_w, k1_t, H, U32)
+        xq_s = gather_codes("xq_s", x_table_s, offs_t, S, U8)
+        xq_w = gather_codes("xq_w", x_table_w, offs_t, S, U32)
+        d_w = deal("d_w", d_picked_w, U32)
+
+        n2_t = load_list("n2_t", n2)
+        n3_t = load_list("n3_t", n3)
+        hz_t = load_list("hz_t", hz)
+        gain = tile("gain", [P, PACK], F32)
+        nc.sync.dma_start(gain[:], gn.rearrange("(p t) o -> p (t o)", t=PACK))
+        n4_t = load_list("n4_t", n4)
+        n5_t = load_list("n5_t", n5)
+        w_w = tile("w_w", [P, 2 * N], U32, tag="d_table_w")
+        w_s = tile("w_s", [P, 2 * N], U8, tag="d_picked_w")
+        nc.gpsimd.memset(w_s[:].bitcast(I32), 0)
+        for j, (words, scales) in enumerate(((w2_words, w2_scales), (w1_words, w1_scales))):
+            nc.sync.dma_start(w_w[:, j * N : (j + 1) * N].bitcast(I32), words[0].rearrange("p n t -> p (n t)").bitcast(I32))
+            for r in range(4):
+                nc.sync.dma_start(w_s[r:P:32, j * N : (j + 1) * N].bitcast(I32), scales[0].bitcast(I32)[r:16:4, :])
+
+        def mx_pass(acc, lhs_w, lhs_s, rhs_w, rhs_s, start, stop):
+            nc.tensor.matmul_mx(
+                out=acc, lhsT=lhs_w.bitcast(FP8X4), lhsT_scale=lhs_s,
+                rhs=rhs_w.bitcast(FP8X4), rhs_scale=rhs_s, start=start, stop=stop,
+            )
+
+        h = []
+        for t in range(TILES):
+            acc = psum.tile([P, S], F32, name=f"h_acc{t}", tag=f"bank{t}")
+            cols = slice(t * P, (t + 1) * P)
+            mx_pass(acc[:], d_w[:, cols], d_s[:, cols], xq_w[:], xq_s[:], True, True)
+            h_t = tile(f"h{t}", [P, S], F32)
+            if t == 0:
+                nc.scalar.activation(h_t[:], acc[:], COPY, scale=0.0625)
+            else:
+                nc.vector.tensor_scalar(h_t[:], acc[:], 0.0625, None, ALU.mult)
+            h.append(h_t)
+
+        neg_gain = tile("neg_gain", [P, PACK], F32)
+        nc.vector.tensor_scalar(neg_gain[:], gain[:], -1.0, None, ALU.mult)
+
+        def fetch(name, window, offsets):
+            dst = tile(name, [P, W], F32)
+            nc.scalar.activation(dst[:], window[:].indirect(offsets), COPY)
+            return dst
+
+        def put(window, offsets, values):
+            nc.scalar.activation(window[:].indirect(offsets[:]), values[:], COPY)
+
+        larger = {}
+        neg_ds = {}
+        z = [tile(f"z{a}", [P, HALF, PACK], BF16) for a in range(2)]
+
+        def pair_up(t):
+            pa = fetch(f"pa{t}", h[t], n1_t[:])
+            pb = fetch(f"pb{t}", h[t], n2_t[:])
+            larger[t] = tile(f"ra{t}", [P, W], F32)
+            nc.vector.tensor_tensor(larger[t][:], pa[:], pb[:], ALU.max)
+
+        def fill(t):
+            put(h[t], n1_t, larger[t])
+            neg_ds[t] = tile(f"neg_ds{t}", [P, S], F32)
+            nc.vector.tensor_scalar(neg_ds[t][:], h[t][:], neg_gain[:, t : t + 1], None, ALU.mult)
+
+        def difference(t, a):
+            other = fetch(f"other{t}_{a}", h[t], n3_t[:, a * 8 : (a + 1) * 8])
+            nc.vector.scalar_tensor_tensor(
+                z[a][:, :, t], other[:], neg_gain[:, t : t + 1], neg_ds[t][:, a * HALF : (a + 1) * HALF],
+                ALU.mult, ALU.subtract,
+            )
+
+        pair_up(0)
+        pair_up(1)
+
+        xh_picked_s = gather_codes("xh_picked_s", x_table_s, hz_t, S, U8)
+        xh_s = tile("xh_s", [P, S], U8)
+        nc.vector.tensor_copy(xh_s[:].bitcast(I32), xh_picked_s[:].bitcast(I32))
+        for e in range(2):
+            nc.sync.dma_start(xh_s[2 + e : P : 32, :].bitcast(I32), xh_s[16 + e : P : 32, :].bitcast(I32))
+        xh_w = gather_codes("xh_w", x_table_w, hz_t, S, U32)
+
+        fill(0)
+        pair_up(2)
+        fill(1)
+        difference(0, 0)
+        pair_up(3)
+        fill(2)
+        difference(1, 0)
+        fill(3)
+        difference(2, 0)
+        difference(0, 1)
+        difference(3, 0)
+
+        h2 = [tile(f"h2_{u}", [P, S], F32) for u in range(TILES)]
+        acc2 = {}
+        for a in range(2):
+            for u in range(TILES):
+                acc2[a, u] = psum.tile([P, HALF], F32, name=f"h2_acc{a}_{u}", tag=f"bank{4 * a + u}")
+                rows = slice(u * P, (u + 1) * P)
+                cols = slice(a * HALF, (a + 1) * HALF)
+                mx_pass(acc2[a, u][:], w_w[:, rows], w_s[:, rows], xh_w[:, cols], xh_s[:, cols], True, False)
+
+        def second_layer(a):
+            z_w = tile(f"z_w{a}", [P, HALF], U32)
+            z_s = tile(f"z_s{a}", [P, HALF], U8)
+            nc.vector.quantize_mx(out=z_w[:].bitcast(FP8X4), scales=z_s[:], in_=z[a][:].rearrange("p j t -> p (j t)"))
+            for u in range(TILES):
+                mx_pass(acc2[a, u][:], w_w[:, N + u * P : N + (u + 1) * P], w_s[:, N + u * P : N + (u + 1) * P], z_w[:], z_s[:], False, True)
+                dst = h2[u][:, a * HALF : (a + 1) * HALF]
+                if a == 1 and u == 0:
+                    nc.scalar.activation(dst, acc2[a, u][:], COPY)
+                else:
+                    nc.vector.tensor_copy(dst, acc2[a, u][:])
+
+        second_layer(0)
+        difference(1, 1)
+        difference(2, 1)
+        difference(3, 1)
+        second_layer(1)
+
+        larger2 = {}
+        ratio = {}
+        result = [tile(f"result{u}", [P, S], F32) for u in range(TILES)]
+
+        def pair_up2(u):
+            pa = fetch(f"pa2_{u}", h2[u], n4_t[:])
+            pb = fetch(f"pb2_{u}", h2[u], n5_t[:])
+            larger2[u] = tile(f"rb{u}", [P, W], F32)
+            nc.vector.tensor_tensor(larger2[u][:], pa[:], pb[:], ALU.max)
+            minus = tile(f"minus{u}", [P, W], F32)
+            nc.vector.tensor_scalar(minus[:], pb[:], -1.0, 0.5, ALU.mult, ALU.add)
+            divisor = tile(f"divisor{u}", [P, W], F32)
+            nc.vector.scalar_tensor_tensor(divisor[:], pb[:], 0.5, minus[:], ALU.add, ALU.max)
+            inverse = tile(f"inverse{u}", [P, W], F32)
+            nc.vector.reciprocal(inverse[:], divisor[:])
+            ratio[u] = tile(f"ratio{u}", [P, W], F32)
+            nc.vector.tensor_tensor(ratio[u][:], pa[:], inverse[:], ALU.mult)
+
+        def finish(u):
+            put(result[u], n4_t, ratio[u])
+            nc.sync.dma_start(out[u * P : (u + 1) * P, :], result[u][:])
+
+        pair_up2(0)
+        pair_up2(1)
+        put(result[0], n5_t, larger2[0])
+        pair_up2(2)
+        pair_up2(3)
+        put(result[1], n5_t, larger2[1])
+        finish(0)
+        put(result[2], n5_t, larger2[2])
+        finish(1)
+        put(result[3], n5_t, larger2[3])
+        finish(2)
+        finish(3)

@@ -19,6 +19,9 @@ P = 128
 PACK = 4
 TILES = 4
 HALF = S // 2
+EARLY = 384
+LAST = S - 64
+SPARE = 16
 
 
 def tile_picked_pqmhfillmratio_none_p_kernel(
@@ -43,8 +46,8 @@ def tile_picked_pqmhfillmratio_none_p_kernel(
             nc.sync.dma_start(dst[:].bitcast(I32), src[0].rearrange("p n t -> p (n t)").bitcast(I32))
             return dst
 
-        def gather_codes(name, table, offsets, count, dtype):
-            dst = tile(name, [P, count], dtype)
+        def gather_codes(name, table, offsets, count, dtype, tag=""):
+            dst = tile(name, [P, count], dtype, tag)
             nc.vector.tensor_copy(dst[:], table[:].indirect(offsets[:]))
             return dst
 
@@ -52,13 +55,11 @@ def tile_picked_pqmhfillmratio_none_p_kernel(
             for e in range(2):
                 nc.scalar.dma_start(plane[2 + e : P : 32, :].bitcast(I32), plane[16 + e : P : 32, :].bitcast(I32))
 
-        def deal(name, src, dtype):
-            dst = tile(name, [P, H], dtype)
+        def deal(dst, src, first, last):
             nc.vector.tensor_copy(
-                dst[:].rearrange("p (t c i) -> p c t i", t=PACK, i=4),
-                src[:].rearrange("p (c i t) -> p c t i", t=PACK, i=4),
+                dst[:].rearrange("p (t c i) -> p c t i", t=last - first, i=4),
+                src[:].rearrange("p (c i t) -> p c t i", t=PACK, i=4)[:, :, first:last, :],
             )
-            return dst
 
         d_table_s = tile("d_table_s", [P, G], U8)
         x_table_s = tile("x_table_s", [P, T], U8)
@@ -68,11 +69,13 @@ def tile_picked_pqmhfillmratio_none_p_kernel(
             nc.gpsimd.memset(table[:, half:].bitcast(I32), 0)
 
         k1_t = load_list("k1_t", k1)
+        d_table_w = tile("d_table_w", [P, G], U32)
+        d_rows = d_words[0].rearrange("p n t -> p (n t)").bitcast(I32)
+        nc.sync.dma_start(d_table_w[:, :EARLY].bitcast(I32), d_rows[:, :EARLY])
         offs_t = load_list("offs_t", offs)
-        n1_t = load_list("n1_t", n1)
         for e in range(2):
             nc.sync.dma_start(d_table_s[e:P:16, :].bitcast(I32), d_scales[0].bitcast(I32)[e:16:2, :])
-        d_table_w = load_words("d_table_w", d_words)
+        nc.sync.dma_start(d_table_w[:, EARLY:].bitcast(I32), d_rows[:, EARLY:])
         for e in range(2):
             nc.sync.dma_start(x_table_s[e:P:16, :].bitcast(I32), x_scales[0].bitcast(I32)[e:16:2, :])
         for e in range(2):
@@ -80,13 +83,16 @@ def tile_picked_pqmhfillmratio_none_p_kernel(
         x_table_w = load_words("x_table_w", x_words)
 
         d_picked_s = gather_codes("d_picked_s", d_table_s, k1_t, H, U8)
-        d_s = deal("d_s", d_picked_s, U8)
+        d_s = tile("d_s", [P, H], U8)
+        deal(d_s, d_picked_s, 0, TILES)
         place_odd_runs(d_s)
         d_picked_w = gather_codes("d_picked_w", d_table_w, k1_t, H, U32)
         xq_s = gather_codes("xq_s", x_table_s, offs_t, S, U8)
         xq_w = gather_codes("xq_w", x_table_w, offs_t, S, U32)
-        d_w = deal("d_w", d_picked_w, U32)
+        d_w = tile("d_w", [P, H], U32)
+        deal(d_w, d_picked_w, 0, TILES)
 
+        n1_t = load_list("n1_t", n1)
         n2_t = load_list("n2_t", n2)
         n3_t = load_list("n3_t", n3)
         hz_t = load_list("hz_t", hz)
@@ -110,14 +116,23 @@ def tile_picked_pqmhfillmratio_none_p_kernel(
 
         h = []
         for t in range(TILES):
-            acc = psum.tile([P, S], F32, name=f"h_acc{t}", tag=f"bank{t}")
-            cols = slice(t * P, (t + 1) * P)
-            mx_pass(acc[:], d_w[:, cols], d_s[:, cols], xq_w[:], xq_s[:], True, True)
-            h_t = tile(f"h{t}", [P, S], F32)
+            rows = slice(t * P, (t + 1) * P)
+            h_t = tile(f"h{t}", [P, S + SPARE if t < 2 else S], F32)
+            if t < 2:
+                nc.gpsimd.memset(h_t[:, S:], 0.0)
             if t == 0:
-                nc.scalar.activation(h_t[:], acc[:], COPY, scale=0.0625)
+                for a in range(2):
+                    cols = slice(a * HALF, (a + 1) * HALF)
+                    acc = psum.tile([P, HALF], F32, name=f"h_acc0_{a}", tag=f"bank{4 * a}")
+                    mx_pass(acc[:], d_w[:, rows], d_s[:, rows], xq_w[:, cols], xq_s[:, cols], True, True)
+                    if a == 0:
+                        nc.scalar.activation(h_t[:, cols], acc[:], COPY, scale=0.0625)
+                    else:
+                        nc.vector.tensor_scalar(h_t[:, cols], acc[:], 0.0625, None, ALU.mult)
             else:
-                nc.vector.tensor_scalar(h_t[:], acc[:], 0.0625, None, ALU.mult)
+                acc = psum.tile([P, S], F32, name=f"h_acc{t}", tag=f"bank{t}")
+                mx_pass(acc[:], d_w[:, rows], d_s[:, rows], xq_w[:], xq_s[:], True, True)
+                nc.vector.tensor_scalar(h_t[:, :S], acc[:], 0.0625, None, ALU.mult)
             h.append(h_t)
 
         neg_gain = tile("neg_gain", [P, PACK], F32)
@@ -133,7 +148,9 @@ def tile_picked_pqmhfillmratio_none_p_kernel(
 
         larger = {}
         neg_ds = {}
-        z = [tile(f"z{a}", [P, HALF, PACK], BF16) for a in range(2)]
+        z = tile("z", [P, S, PACK], BF16)
+        z_w = tile("z_w", [P, S], U32)
+        z_s = tile("z_s", [P, S], U8)
 
         def pair_up(t):
             pa = fetch(f"pa{t}", h[t], n1_t[:])
@@ -144,36 +161,41 @@ def tile_picked_pqmhfillmratio_none_p_kernel(
         def fill(t):
             put(h[t], n1_t, larger[t])
             neg_ds[t] = tile(f"neg_ds{t}", [P, S], F32)
-            nc.vector.tensor_scalar(neg_ds[t][:], h[t][:], neg_gain[:, t : t + 1], None, ALU.mult)
+            nc.vector.tensor_scalar(neg_ds[t][:], h[t][:, :S], neg_gain[:, t : t + 1], None, ALU.mult)
 
-        def difference(t, a):
-            other = fetch(f"other{t}_{a}", h[t], n3_t[:, a * 8 : (a + 1) * 8])
+        def difference(t, lo, hi):
+            other = tile(f"other{t}_{lo}", [P, hi - lo], F32)
+            nc.scalar.activation(other[:], h[t][:].indirect(n3_t[:, lo // 16 : hi // 16]), COPY)
             nc.vector.scalar_tensor_tensor(
-                z[a][:, :, t], other[:], neg_gain[:, t : t + 1], neg_ds[t][:, a * HALF : (a + 1) * HALF],
-                ALU.mult, ALU.subtract,
+                z[:, lo:hi, t], other[:], neg_gain[:, t : t + 1], neg_ds[t][:, lo:hi], ALU.mult, ALU.subtract,
+            )
+
+        def quantise(lo, hi):
+            nc.vector.quantize_mx(
+                out=z_w[:, lo:hi].bitcast(FP8X4), scales=z_s[:, lo:hi], in_=z[:, lo:hi, :].rearrange("p j t -> p (j t)"),
             )
 
         pair_up(0)
         pair_up(1)
 
-        xh_picked_s = gather_codes("xh_picked_s", x_table_s, hz_t, S, U8)
+        xh_picked_s = gather_codes("xh_picked_s", x_table_s, hz_t, S, U8, tag="d_w")
         xh_s = tile("xh_s", [P, S], U8)
         nc.vector.tensor_copy(xh_s[:].bitcast(I32), xh_picked_s[:].bitcast(I32))
         for e in range(2):
             nc.sync.dma_start(xh_s[2 + e : P : 32, :].bitcast(I32), xh_s[16 + e : P : 32, :].bitcast(I32))
-        xh_w = gather_codes("xh_w", x_table_w, hz_t, S, U32)
+        xh_w = gather_codes("xh_w", x_table_w, hz_t, S, U32, tag="xq_w")
 
         fill(0)
         pair_up(2)
         fill(1)
-        difference(0, 0)
+        difference(0, 0, S)
         pair_up(3)
         fill(2)
-        difference(1, 0)
+        difference(1, 0, S)
+        difference(2, 0, HALF)
         fill(3)
-        difference(2, 0)
-        difference(0, 1)
-        difference(3, 0)
+        difference(2, HALF, S)
+        difference(3, 0, HALF)
 
         h2 = [tile(f"h2_{u}", [P, S], F32) for u in range(TILES)]
         acc2 = {}
@@ -184,23 +206,22 @@ def tile_picked_pqmhfillmratio_none_p_kernel(
                 cols = slice(a * HALF, (a + 1) * HALF)
                 mx_pass(acc2[a, u][:], w_w[:, rows], w_s[:, rows], xh_w[:, cols], xh_s[:, cols], True, False)
 
-        def second_layer(a):
-            z_w = tile(f"z_w{a}", [P, HALF], U32)
-            z_s = tile(f"z_s{a}", [P, HALF], U8)
-            nc.vector.quantize_mx(out=z_w[:].bitcast(FP8X4), scales=z_s[:], in_=z[a][:].rearrange("p j t -> p (j t)"))
-            for u in range(TILES):
-                mx_pass(acc2[a, u][:], w_w[:, N + u * P : N + (u + 1) * P], w_s[:, N + u * P : N + (u + 1) * P], z_w[:], z_s[:], False, True)
-                dst = h2[u][:, a * HALF : (a + 1) * HALF]
-                if a == 1 and u == 0:
-                    nc.scalar.activation(dst, acc2[a, u][:], COPY)
-                else:
-                    nc.vector.tensor_copy(dst, acc2[a, u][:])
+        def second_layer(a, u):
+            cols = slice(a * HALF, (a + 1) * HALF)
+            mx_pass(acc2[a, u][:], w_w[:, N + u * P : N + (u + 1) * P], w_s[:, N + u * P : N + (u + 1) * P], z_w[:, cols], z_s[:, cols], False, True)
+            if a == 1 and u == 0:
+                nc.scalar.activation(h2[u][:, cols], acc2[a, u][:], COPY)
+            else:
+                nc.vector.tensor_copy(h2[u][:, cols], acc2[a, u][:])
 
-        second_layer(0)
-        difference(1, 1)
-        difference(2, 1)
-        difference(3, 1)
-        second_layer(1)
+        difference(3, HALF, LAST)
+        quantise(0, HALF)
+        difference(3, LAST, S)
+        quantise(HALF, LAST)
+        quantise(LAST, S)
+        for u in range(TILES):
+            for a in range(2):
+                second_layer(a, u)
 
         larger2 = {}
         ratio = {}

@@ -20,8 +20,7 @@ PACK = 4
 TILES = 4
 HALF = S // 2
 EARLY = 384
-LAST = S - 64
-SPARE = 16
+PIECE = 64
 
 
 def tile_picked_pqmhfillmratio_none_p_kernel(
@@ -62,8 +61,9 @@ def tile_picked_pqmhfillmratio_none_p_kernel(
             )
 
         d_table_s = tile("d_table_s", [P, G], U8)
-        x_table_s = tile("x_table_s", [P, T], U8)
-        for table in (d_table_s, x_table_s):
+        xq_table_s = tile("xq_table_s", [P, T], U8)
+        xh_table_s = tile("xh_table_s", [P, T], U8)
+        for table in (d_table_s, xq_table_s, xh_table_s):
             half = table.shape[1] // 2
             nc.vector.memset(table[:, :half].bitcast(I32), 0)
             nc.gpsimd.memset(table[:, half:].bitcast(I32), 0)
@@ -76,26 +76,28 @@ def tile_picked_pqmhfillmratio_none_p_kernel(
         for e in range(2):
             nc.sync.dma_start(d_table_s[e:P:16, :].bitcast(I32), d_scales[0].bitcast(I32)[e:16:2, :])
         nc.sync.dma_start(d_table_w[:, EARLY:].bitcast(I32), d_rows[:, EARLY:])
-        for e in range(2):
-            nc.sync.dma_start(x_table_s[e:P:16, :].bitcast(I32), x_scales[0].bitcast(I32)[e:16:2, :])
-        for e in range(2):
-            nc.sync.dma_start(x_table_s[2 + e : P : 32, :].bitcast(I32), x_scales[0].bitcast(I32)[2 + e : 16 : 4, :])
         x_table_w = load_words("x_table_w", x_words)
+        for r in range(4):
+            nc.sync.dma_start(xq_table_s[r:P:32, :].bitcast(I32), x_scales[0].bitcast(I32)[r:16:4, :])
 
         d_picked_s = gather_codes("d_picked_s", d_table_s, k1_t, H, U8)
         d_s = tile("d_s", [P, H], U8)
         deal(d_s, d_picked_s, 0, TILES)
         place_odd_runs(d_s)
         d_picked_w = gather_codes("d_picked_w", d_table_w, k1_t, H, U32)
-        xq_s = gather_codes("xq_s", x_table_s, offs_t, S, U8)
+        d_w_first = tile("d_w_first", [P, P], U32)
+        deal(d_w_first, d_picked_w, 0, 1)
         xq_w = gather_codes("xq_w", x_table_w, offs_t, S, U32)
-        d_w = tile("d_w", [P, H], U32)
-        deal(d_w, d_picked_w, 0, TILES)
+        xq_s = gather_codes("xq_s", xq_table_s, offs_t, S, U8)
+        d_w_rest = tile("d_w_rest", [P, H - P], U32, tag="xq_table_s")
+        deal(d_w_rest, d_picked_w, 1, TILES)
 
         n1_t = load_list("n1_t", n1)
         n2_t = load_list("n2_t", n2)
         n3_t = load_list("n3_t", n3)
         hz_t = load_list("hz_t", hz)
+        for e in range(2):
+            nc.sync.dma_start(xh_table_s[e:P:16, :].bitcast(I32), x_scales[0].bitcast(I32)[e:16:2, :])
         gain = tile("gain", [P, PACK], F32)
         nc.sync.dma_start(gain[:], gn.rearrange("(p t) o -> p (t o)", t=PACK))
         n4_t = load_list("n4_t", n4)
@@ -117,26 +119,21 @@ def tile_picked_pqmhfillmratio_none_p_kernel(
         h = []
         for t in range(TILES):
             rows = slice(t * P, (t + 1) * P)
-            h_t = tile(f"h{t}", [P, S + SPARE if t < 2 else S], F32)
-            if t < 2:
-                nc.gpsimd.memset(h_t[:, S:], 0.0)
+            h_t = tile(f"h{t}", [P, S], F32)
             if t == 0:
                 for a in range(2):
                     cols = slice(a * HALF, (a + 1) * HALF)
                     acc = psum.tile([P, HALF], F32, name=f"h_acc0_{a}", tag=f"bank{4 * a}")
-                    mx_pass(acc[:], d_w[:, rows], d_s[:, rows], xq_w[:, cols], xq_s[:, cols], True, True)
+                    mx_pass(acc[:], d_w_first[:], d_s[:, rows], xq_w[:, cols], xq_s[:, cols], True, True)
                     if a == 0:
                         nc.scalar.activation(h_t[:, cols], acc[:], COPY, scale=0.0625)
                     else:
                         nc.vector.tensor_scalar(h_t[:, cols], acc[:], 0.0625, None, ALU.mult)
             else:
                 acc = psum.tile([P, S], F32, name=f"h_acc{t}", tag=f"bank{t}")
-                mx_pass(acc[:], d_w[:, rows], d_s[:, rows], xq_w[:], xq_s[:], True, True)
-                nc.vector.tensor_scalar(h_t[:, :S], acc[:], 0.0625, None, ALU.mult)
+                mx_pass(acc[:], d_w_rest[:, (t - 1) * P : t * P], d_s[:, rows], xq_w[:], xq_s[:], True, True)
+                nc.vector.tensor_scalar(h_t[:], acc[:], 0.0625, None, ALU.mult)
             h.append(h_t)
-
-        neg_gain = tile("neg_gain", [P, PACK], F32)
-        nc.vector.tensor_scalar(neg_gain[:], gain[:], -1.0, None, ALU.mult)
 
         def fetch(name, window, offsets):
             dst = tile(name, [P, W], F32)
@@ -147,8 +144,9 @@ def tile_picked_pqmhfillmratio_none_p_kernel(
             nc.scalar.activation(window[:].indirect(offsets[:]), values[:], COPY)
 
         larger = {}
-        neg_ds = {}
-        z = tile("z", [P, S, PACK], BF16)
+        gained = tile("gained", [P, TILES, S], F32)
+        partner = [tile(f"partner{a}", [P, TILES, HALF], F32) for a in range(2)]
+        z = [tile(f"z{a}", [P, HALF, PACK], BF16) for a in range(2)]
         z_w = tile("z_w", [P, S], U32)
         z_s = tile("z_s", [P, S], U8)
 
@@ -160,25 +158,30 @@ def tile_picked_pqmhfillmratio_none_p_kernel(
 
         def fill(t):
             put(h[t], n1_t, larger[t])
-            neg_ds[t] = tile(f"neg_ds{t}", [P, S], F32)
-            nc.vector.tensor_scalar(neg_ds[t][:], h[t][:, :S], neg_gain[:, t : t + 1], None, ALU.mult)
+            nc.vector.tensor_scalar(gained[:, t, :], h[t][:], gain[:, t : t + 1], None, ALU.mult)
 
-        def difference(t, lo, hi):
-            other = tile(f"other{t}_{lo}", [P, hi - lo], F32)
-            nc.scalar.activation(other[:], h[t][:].indirect(n3_t[:, lo // 16 : hi // 16]), COPY)
-            nc.vector.scalar_tensor_tensor(
-                z[:, lo:hi, t], other[:], neg_gain[:, t : t + 1], neg_ds[t][:, lo:hi], ALU.mult, ALU.subtract,
+        def fetch_partner(t, a, lo, hi):
+            offsets = n3_t[:, (a * HALF + lo) // 16 : (a * HALF + hi) // 16]
+            nc.scalar.activation(partner[a][:, t, lo:hi], gained[:, t, :].indirect(offsets), COPY)
+
+        def difference(a, lo, hi):
+            nc.vector.tensor_tensor(
+                z[a][:, lo:hi, :].rearrange("p (c i) t -> p c t i", i=4),
+                gained[:, :, a * HALF + lo : a * HALF + hi].rearrange("p t (c i) -> p c t i", i=4),
+                partner[a][:, :, lo:hi].rearrange("p t (c i) -> p c t i", i=4),
+                ALU.subtract,
             )
 
-        def quantise(lo, hi):
+        def quantise(a, lo, hi):
+            cols = slice(a * HALF + lo, a * HALF + hi)
             nc.vector.quantize_mx(
-                out=z_w[:, lo:hi].bitcast(FP8X4), scales=z_s[:, lo:hi], in_=z[:, lo:hi, :].rearrange("p j t -> p (j t)"),
+                out=z_w[:, cols].bitcast(FP8X4), scales=z_s[:, cols], in_=z[a][:, lo:hi, :].rearrange("p j t -> p (j t)"),
             )
 
         pair_up(0)
         pair_up(1)
 
-        xh_picked_s = gather_codes("xh_picked_s", x_table_s, hz_t, S, U8, tag="d_w")
+        xh_picked_s = gather_codes("xh_picked_s", xh_table_s, hz_t, S, U8, tag="xq_table_s")
         xh_s = tile("xh_s", [P, S], U8)
         nc.vector.tensor_copy(xh_s[:].bitcast(I32), xh_picked_s[:].bitcast(I32))
         for e in range(2):
@@ -188,72 +191,69 @@ def tile_picked_pqmhfillmratio_none_p_kernel(
         fill(0)
         pair_up(2)
         fill(1)
-        difference(0, 0, S)
         pair_up(3)
         fill(2)
-        difference(1, 0, S)
-        difference(2, 0, HALF)
         fill(3)
-        difference(2, HALF, S)
-        difference(3, 0, HALF)
+        for t in range(TILES):
+            fetch_partner(t, 0, 0, HALF)
+        difference(0, 0, HALF)
+        for t in range(TILES - 1):
+            fetch_partner(t, 1, 0, HALF)
+        quantise(0, 0, HALF)
 
         h2 = [tile(f"h2_{u}", [P, S], F32) for u in range(TILES)]
-        acc2 = {}
-        for a in range(2):
-            for u in range(TILES):
-                acc2[a, u] = psum.tile([P, HALF], F32, name=f"h2_acc{a}_{u}", tag=f"bank{4 * a + u}")
-                rows = slice(u * P, (u + 1) * P)
-                cols = slice(a * HALF, (a + 1) * HALF)
-                mx_pass(acc2[a, u][:], w_w[:, rows], w_s[:, rows], xh_w[:, cols], xh_s[:, cols], True, False)
+        parts = [(0, slice(0, HALF)), (0, slice(HALF, S))] + [(u, slice(0, S)) for u in range(1, TILES)]
+        acc2 = []
+        for b, (u, cols) in enumerate(parts):
+            acc2.append(psum.tile([P, cols.stop - cols.start], F32, name=f"h2_acc{b}", tag=f"bank{b}"))
+            rows = slice(u * P, (u + 1) * P)
+            mx_pass(acc2[b][:], w_w[:, rows], w_s[:, rows], xh_w[:, cols], xh_s[:, cols], True, False)
 
-        def second_layer(a, u):
-            cols = slice(a * HALF, (a + 1) * HALF)
-            mx_pass(acc2[a, u][:], w_w[:, N + u * P : N + (u + 1) * P], w_s[:, N + u * P : N + (u + 1) * P], z_w[:, cols], z_s[:, cols], False, True)
-            if a == 1 and u == 0:
-                nc.scalar.activation(h2[u][:, cols], acc2[a, u][:], COPY)
+        def second_layer(b):
+            u, cols = parts[b]
+            rows = slice(N + u * P, N + (u + 1) * P)
+            mx_pass(acc2[b][:], w_w[:, rows], w_s[:, rows], z_w[:, cols], z_s[:, cols], False, True)
+            if u == 0:
+                nc.scalar.activation(h2[u][:, cols], acc2[b][:], COPY)
             else:
-                nc.vector.tensor_copy(h2[u][:, cols], acc2[a, u][:])
+                nc.vector.tensor_copy(h2[u][:, cols], acc2[b][:])
 
-        difference(3, HALF, LAST)
-        quantise(0, HALF)
-        difference(3, LAST, S)
-        quantise(HALF, LAST)
-        quantise(LAST, S)
-        for u in range(TILES):
-            for a in range(2):
-                second_layer(a, u)
+        fetch_partner(TILES - 1, 1, 0, PIECE)
+        difference(1, 0, PIECE)
+        fetch_partner(TILES - 1, 1, PIECE, HALF)
+        difference(1, PIECE, HALF)
+        quantise(1, 0, PIECE)
+        quantise(1, PIECE, HALF)
+        for b in range(len(parts)):
+            second_layer(b)
 
+        pa2 = {}
+        pb2 = {}
         larger2 = {}
         ratio = {}
         result = [tile(f"result{u}", [P, S], F32) for u in range(TILES)]
 
         def pair_up2(u):
-            pa = fetch(f"pa2_{u}", h2[u], n4_t[:])
-            pb = fetch(f"pb2_{u}", h2[u], n5_t[:])
+            pa2[u] = fetch(f"pa2_{u}", h2[u], n4_t[:])
+            pb2[u] = fetch(f"pb2_{u}", h2[u], n5_t[:])
             larger2[u] = tile(f"rb{u}", [P, W], F32)
-            nc.vector.tensor_tensor(larger2[u][:], pa[:], pb[:], ALU.max)
+            nc.vector.tensor_tensor(larger2[u][:], pa2[u][:], pb2[u][:], ALU.max)
+
+        def divide(u):
             minus = tile(f"minus{u}", [P, W], F32)
-            nc.vector.tensor_scalar(minus[:], pb[:], -1.0, 0.5, ALU.mult, ALU.add)
+            nc.vector.tensor_scalar(minus[:], pb2[u][:], -1.0, 0.5, ALU.mult, ALU.add)
             divisor = tile(f"divisor{u}", [P, W], F32)
-            nc.vector.scalar_tensor_tensor(divisor[:], pb[:], 0.5, minus[:], ALU.add, ALU.max)
+            nc.vector.scalar_tensor_tensor(divisor[:], pb2[u][:], 0.5, minus[:], ALU.add, ALU.max)
             inverse = tile(f"inverse{u}", [P, W], F32)
             nc.vector.reciprocal(inverse[:], divisor[:])
             ratio[u] = tile(f"ratio{u}", [P, W], F32)
-            nc.vector.tensor_tensor(ratio[u][:], pa[:], inverse[:], ALU.mult)
+            nc.vector.tensor_tensor(ratio[u][:], pa2[u][:], inverse[:], ALU.mult)
 
-        def finish(u):
+        for u in range(TILES):
+            pair_up2(u)
+        for u in range(TILES):
+            put(result[u], n5_t, larger2[u])
+            divide(u)
+        for u in range(TILES):
             put(result[u], n4_t, ratio[u])
             nc.sync.dma_start(out[u * P : (u + 1) * P, :], result[u][:])
-
-        pair_up2(0)
-        pair_up2(1)
-        put(result[0], n5_t, larger2[0])
-        pair_up2(2)
-        pair_up2(3)
-        put(result[1], n5_t, larger2[1])
-        finish(0)
-        put(result[2], n5_t, larger2[2])
-        finish(1)
-        put(result[3], n5_t, larger2[3])
-        finish(2)
-        finish(3)

@@ -103,7 +103,7 @@ def tile_picked_pqmhfillmratio_none_p_kernel(
         n4_t = load_list("n4_t", n4)
         n5_t = load_list("n5_t", n5)
         w_w = tile("w_w", [P, 2 * N], U32, tag="d_table_w")
-        w_s = tile("w_s", [P, 2 * N], U8, tag="d_picked_w")
+        w_s = tile("w_s", [P, 2 * N], U8, tag="d_picked_s")
         nc.gpsimd.memset(w_s[:].bitcast(I32), 0)
         for j, (words, scales) in enumerate(((w2_words, w2_scales), (w1_words, w1_scales))):
             nc.sync.dma_start(w_w[:, j * N : (j + 1) * N].bitcast(I32), words[0].rearrange("p n t -> p (n t)").bitcast(I32))
@@ -249,11 +249,18 @@ def tile_picked_pqmhfillmratio_none_p_kernel(
             ratio[u] = tile(f"ratio{u}", [P, W], F32)
             nc.vector.tensor_tensor(ratio[u][:], pa2[u][:], inverse[:], ALU.mult)
 
-        for u in range(TILES):
-            pair_up2(u)
-        for u in range(TILES):
-            put(result[u], n5_t, larger2[u])
-            divide(u)
-        for u in range(TILES):
+        def finish(u):
             put(result[u], n4_t, ratio[u])
             nc.sync.dma_start(out[u * P : (u + 1) * P, :], result[u][:])
+
+        for u in range(2):
+            pair_up2(u)
+            divide(u)
+        put(result[0], n5_t, larger2[0])
+        for u in range(2, TILES):
+            pair_up2(u)
+            divide(u)
+        for u in range(1, TILES):
+            put(result[u], n5_t, larger2[u])
+        for u in range(TILES):
+            finish(u)

from contextlib import ExitStack

import concourse.mybir as mybir

K, T, S, N, G, H, W = 512, 1024, 256, 512, 2048, 512, 128
FLOPS = 2 * S * (K * H + H * N + K * N)

F32 = mybir.dt.float32
BF16 = mybir.dt.bfloat16
I32 = mybir.dt.int32
U32 = mybir.dt.uint32
U16 = mybir.dt.uint16
U8 = mybir.dt.uint8
FP8X4 = mybir.dt.float8_e4m3fn_x4
ALU = mybir.AluOpType
COPY = mybir.ActivationFunctionType.Copy

P = 128
PACK = 4
TILES = 4
HALF = S // 2
EARLY = 384
PIECE = 64


def tile_picked_pqmhfillmratio_none_p_kernel(
    tc, x_words, x_scales, d_words, d_scales, gn, w1_words, w1_scales, w2_words, w2_scales,
    offs, k1, n1, n2, n3, hz, n4, n5, out,
):
    nc = tc.nc
    with ExitStack() as ctx:
        sb = ctx.enter_context(tc.tile_pool(name="sb", bufs=1))
        psum = ctx.enter_context(tc.psum_pool(name="psum", bufs=1))

        def tile(name, shape, dtype, tag=""):
            return sb.tile(shape, dtype, name=name, align_bytes=64, tag=tag or name)

        def load_list(name, src):
            dst = tile(name, list(src.shape), U16)
            nc.sync.dma_start(dst[:], src)
            return dst

        def load_words(name, src):
            dst = tile(name, [P, src.shape[2]], U32)
            nc.sync.dma_start(dst[:].bitcast(I32), src[0].rearrange("p n t -> p (n t)").bitcast(I32))
            return dst

        def gather_codes(name, table, offsets, count, dtype, tag=""):
            dst = tile(name, [P, count], dtype, tag)
            nc.vector.tensor_copy(dst[:], table[:].indirect(offsets[:]))
            return dst

        def place_odd_runs(plane):
            for e in range(2):
                nc.scalar.dma_start(plane[2 + e : P : 32, :].bitcast(I32), plane[16 + e : P : 32, :].bitcast(I32))

        def deal(dst, src, first, last):
            nc.vector.tensor_copy(
                dst[:].rearrange("p (t c i) -> p c t i", t=last - first, i=4),
                src[:].rearrange("p (c i t) -> p c t i", t=PACK, i=4)[:, :, first:last, :],
            )

        d_table_s = tile("d_table_s", [P, G], U8)
        xq_table_s = tile("xq_table_s", [P, T], U8)
        xh_table_s = tile("xh_table_s", [P, T], U8)
        for table in (d_table_s, xq_table_s, xh_table_s):
            half = table.shape[1] // 2
            nc.vector.memset(table[:, :half].bitcast(I32), 0)
            nc.gpsimd.memset(table[:, half:].bitcast(I32), 0)

        k1_t = load_list("k1_t", k1)
        d_table_w = tile("d_table_w", [P, G], U32)
        d_rows = d_words[0].rearrange("p n t -> p (n t)").bitcast(I32)
        nc.sync.dma_start(d_table_w[:, :EARLY].bitcast(I32), d_rows[:, :EARLY])
        offs_t = load_list("offs_t", offs)
        for e in range(2):
            nc.sync.dma_start(d_table_s[e:P:16, :].bitcast(I32), d_scales[0].bitcast(I32)[e:16:2, :])
        nc.sync.dma_start(d_table_w[:, EARLY:].bitcast(I32), d_rows[:, EARLY:])
        x_table_w = load_words("x_table_w", x_words)
        for r in range(4):
            nc.sync.dma_start(xq_table_s[r:P:32, :].bitcast(I32), x_scales[0].bitcast(I32)[r:16:4, :])

        d_picked_s = gather_codes("d_picked_s", d_table_s, k1_t, H, U8)
        d_s = tile("d_s", [P, H], U8)
        deal(d_s, d_picked_s, 0, TILES)
        place_odd_runs(d_s)
        d_picked_w = gather_codes("d_picked_w", d_table_w, k1_t, H, U32)
        d_w_first = tile("d_w_first", [P, P], U32)
        deal(d_w_first, d_picked_w, 0, 1)
        xq_w = gather_codes("xq_w", x_table_w, offs_t, S, U32)
        xq_s = gather_codes("xq_s", xq_table_s, offs_t, S, U8)
        d_w_rest = tile("d_w_rest", [P, H - P], U32, tag="xq_table_s")
        deal(d_w_rest, d_picked_w, 1, TILES)

        n1_t = load_list("n1_t", n1)
        n2_t = load_list("n2_t", n2)
        n3_t = load_list("n3_t", n3)
        hz_t = load_list("hz_t", hz)
        for e in range(2):
            nc.sync.dma_start(xh_table_s[e:P:16, :].bitcast(I32), x_scales[0].bitcast(I32)[e:16:2, :])
        gain = tile("gain", [P, PACK], F32)
        nc.sync.dma_start(gain[:], gn.rearrange("(p t) o -> p (t o)", t=PACK))
        n4_t = load_list("n4_t", n4)
        n5_t = load_list("n5_t", n5)
        w_w = tile("w_w", [P, 2 * N], U32, tag="d_table_w")
        w_s = tile("w_s", [P, 2 * N], U8, tag="d_picked_s")
        nc.gpsimd.memset(w_s[:].bitcast(I32), 0)
        for j, (words, scales) in enumerate(((w2_words, w2_scales), (w1_words, w1_scales))):
            nc.sync.dma_start(w_w[:, j * N : (j + 1) * N].bitcast(I32), words[0].rearrange("p n t -> p (n t)").bitcast(I32))
            for r in range(4):
                nc.sync.dma_start(w_s[r:P:32, j * N : (j + 1) * N].bitcast(I32), scales[0].bitcast(I32)[r:16:4, :])

        def mx_pass(acc, lhs_w, lhs_s, rhs_w, rhs_s, start, stop):
            nc.tensor.matmul_mx(
                out=acc, lhsT=lhs_w.bitcast(FP8X4), lhsT_scale=lhs_s,
                rhs=rhs_w.bitcast(FP8X4), rhs_scale=rhs_s, start=start, stop=stop,
            )

        h = []
        for t in range(TILES):
            rows = slice(t * P, (t + 1) * P)
            h_t = tile(f"h{t}", [P, S], F32)
            if t == 0:
                for a in range(2):
                    cols = slice(a * HALF, (a + 1) * HALF)
                    acc = psum.tile([P, HALF], F32, name=f"h_acc0_{a}", tag=f"bank{4 * a}")
                    mx_pass(acc[:], d_w_first[:], d_s[:, rows], xq_w[:, cols], xq_s[:, cols], True, True)
                    if a == 0:
                        nc.scalar.activation(h_t[:, cols], acc[:], COPY, scale=0.0625)
                    else:
                        nc.vector.tensor_scalar(h_t[:, cols], acc[:], 0.0625, None, ALU.mult)
            else:
                acc = psum.tile([P, S], F32, name=f"h_acc{t}", tag=f"bank{t}")
                mx_pass(acc[:], d_w_rest[:, (t - 1) * P : t * P], d_s[:, rows], xq_w[:], xq_s[:], True, True)
                nc.vector.tensor_scalar(h_t[:], acc[:], 0.0625, None, ALU.mult)
            h.append(h_t)

        def fetch(name, window, offsets):
            dst = tile(name, [P, W], F32)
            nc.scalar.activation(dst[:], window[:].indirect(offsets), COPY)
            return dst

        def put(window, offsets, values):
            nc.scalar.activation(window[:].indirect(offsets[:]), values[:], COPY)

        larger = {}
        gained = tile("gained", [P, TILES, S], F32)
        partner = [tile(f"partner{a}", [P, TILES, HALF], F32) for a in range(2)]
        z = [tile(f"z{a}", [P, HALF, PACK], BF16) for a in range(2)]
        z_w = tile("z_w", [P, S], U32)
        z_s = tile("z_s", [P, S], U8)

        def pair_up(t):
            pa = fetch(f"pa{t}", h[t], n1_t[:])
            pb = fetch(f"pb{t}", h[t], n2_t[:])
            larger[t] = tile(f"ra{t}", [P, W], F32)
            nc.vector.tensor_tensor(larger[t][:], pa[:], pb[:], ALU.max)

        def fill(t):
            put(h[t], n1_t, larger[t])
            nc.vector.tensor_scalar(gained[:, t, :], h[t][:], gain[:, t : t + 1], None, ALU.mult)

        def fetch_partner(t, a, lo, hi):
            offsets = n3_t[:, (a * HALF + lo) // 16 : (a * HALF + hi) // 16]
            nc.scalar.activation(partner[a][:, t, lo:hi], gained[:, t, :].indirect(offsets), COPY)

        def difference(a, lo, hi):
            nc.vector.tensor_tensor(
                z[a][:, lo:hi, :].rearrange("p (c i) t -> p c t i", i=4),
                gained[:, :, a * HALF + lo : a * HALF + hi].rearrange("p t (c i) -> p c t i", i=4),
                partner[a][:, :, lo:hi].rearrange("p t (c i) -> p c t i", i=4),
                ALU.subtract,
            )

        def quantise(a, lo, hi):
            cols = slice(a * HALF + lo, a * HALF + hi)
            nc.vector.quantize_mx(
                out=z_w[:, cols].bitcast(FP8X4), scales=z_s[:, cols], in_=z[a][:, lo:hi, :].rearrange("p j t -> p (j t)"),
            )

        pair_up(0)
        pair_up(1)

        xh_picked_s = gather_codes("xh_picked_s", xh_table_s, hz_t, S, U8, tag="xq_table_s")
        xh_s = tile("xh_s", [P, S], U8)
        nc.vector.tensor_copy(xh_s[:].bitcast(I32), xh_picked_s[:].bitcast(I32))
        for e in range(2):
            nc.sync.dma_start(xh_s[2 + e : P : 32, :].bitcast(I32), xh_s[16 + e : P : 32, :].bitcast(I32))
        xh_w = gather_codes("xh_w", x_table_w, hz_t, S, U32, tag="xq_w")

        fill(0)
        pair_up(2)
        fill(1)
        pair_up(3)
        fill(2)
        fill(3)
        for t in range(TILES):
            fetch_partner(t, 0, 0, HALF)
        difference(0, 0, HALF)
        for t in range(TILES - 1):
            fetch_partner(t, 1, 0, HALF)
        quantise(0, 0, HALF)

        h2 = [tile(f"h2_{u}", [P, S], F32) for u in range(TILES)]
        parts = [(0, slice(0, HALF)), (0, slice(HALF, S))] + [(u, slice(0, S)) for u in range(1, TILES)]
        acc2 = []
        for b, (u, cols) in enumerate(parts):
            acc2.append(psum.tile([P, cols.stop - cols.start], F32, name=f"h2_acc{b}", tag=f"bank{b}"))
            rows = slice(u * P, (u + 1) * P)
            mx_pass(acc2[b][:], w_w[:, rows], w_s[:, rows], xh_w[:, cols], xh_s[:, cols], True, False)

        def second_layer(b):
            u, cols = parts[b]
            rows = slice(N + u * P, N + (u + 1) * P)
            mx_pass(acc2[b][:], w_w[:, rows], w_s[:, rows], z_w[:, cols], z_s[:, cols], False, True)
            if u == 0:
                nc.scalar.activation(h2[u][:, cols], acc2[b][:], COPY)
            else:
                nc.vector.tensor_copy(h2[u][:, cols], acc2[b][:])

        fetch_partner(TILES - 1, 1, 0, PIECE)
        difference(1, 0, PIECE)
        fetch_partner(TILES - 1, 1, PIECE, HALF)
        difference(1, PIECE, HALF)
        quantise(1, 0, PIECE)
        quantise(1, PIECE, HALF)
        for b in range(len(parts)):
            second_layer(b)

        pa2 = {}
        pb2 = {}
        larger2 = {}
        ratio = {}
        result = [tile(f"result{u}", [P, S], F32) for u in range(TILES)]

        def pair_up2(u):
            pa2[u] = fetch(f"pa2_{u}", h2[u], n4_t[:])
            pb2[u] = fetch(f"pb2_{u}", h2[u], n5_t[:])
            larger2[u] = tile(f"rb{u}", [P, W], F32)
            nc.vector.tensor_tensor(larger2[u][:], pa2[u][:], pb2[u][:], ALU.max)

        def divide(u):
            minus = tile(f"minus{u}", [P, W], F32)
            nc.vector.tensor_scalar(minus[:], pb2[u][:], -1.0, 0.5, ALU.mult, ALU.add)
            divisor = tile(f"divisor{u}", [P, W], F32)
            nc.vector.scalar_tensor_tensor(divisor[:], pb2[u][:], 0.5, minus[:], ALU.add, ALU.max)
            inverse = tile(f"inverse{u}", [P, W], F32)
            nc.vector.reciprocal(inverse[:], divisor[:])
            ratio[u] = tile(f"ratio{u}", [P, W], F32)
            nc.vector.tensor_tensor(ratio[u][:], pa2[u][:], inverse[:], ALU.mult)

        def finish(u):
            put(result[u], n4_t, ratio[u])
            nc.sync.dma_start(out[u * P : (u + 1) * P, :], result[u][:])

        for u in range(2):
            pair_up2(u)
            divide(u)
        put(result[0], n5_t, larger2[0])
        for u in range(2, TILES):
            pair_up2(u)
            divide(u)
        for u in range(1, TILES):
            put(result[u], n5_t, larger2[u])
        for u in range(TILES):
            finish(u)
